import numpy as np
import ml_dtypes


def mxq(x, axis, fmt="e4m3"):
    dtype, down = {"e4m3": (ml_dtypes.float8_e4m3fn, 7), "e5m2": (ml_dtypes.float8_e5m2, 14)}[fmt]
    v = np.moveaxis(np.asarray(x, np.float32).astype(ml_dtypes.bfloat16).astype(np.float64), axis, -1)
    blocks = v.reshape(v.shape[:-1] + (-1, 32))
    amax = np.abs(blocks).max(-1, keepdims=True)
    byte = np.maximum(np.where(amax > 0, np.frexp(amax)[1] - 1 + 127, 0) - down, 1)
    scale = np.exp2(byte - 127.0)
    codes = (blocks / scale).astype(np.float32).astype(dtype).astype(np.float64)
    return np.moveaxis((codes * scale).reshape(v.shape), -1, axis)


WIDE = False


def mx_kscale(k):
    if not WIDE:
        return np.ones(k)
    levels = np.array([10, -10, 5, -5, 0])
    if k % 512:
        return np.exp2(np.random.permutation(np.resize(levels, k // 32))).repeat(32)
    a = np.empty((k // 512, 16))
    for p in range(k // 512):
        a[p, :8] = np.random.permutation(np.resize(levels, 8))
        for g in range(8):
            far = levels[np.abs(levels - a[p, g]) >= 10]
            a[p, g + 8] = far[np.random.randint(len(far))]
    return np.exp2(a.ravel()).repeat(32)


BF16 = ml_dtypes.bfloat16


def bf(x):
    return np.asarray(x, np.float32).astype(BF16)


def f64(x):
    return np.asarray(x).astype(np.float64)


E2M1 = np.array([0.0, 0.5, 1.0, 1.5, 2.0, 3.0, 4.0, 6.0, -0.0, -0.5, -1.0, -1.5, -2.0, -3.0, -4.0, -6.0])


def pack_weight(w, fmt):
    k, n = w.shape
    w = f64(bf(w)).reshape(k // 32, 32, n)
    amax = np.abs(w).max(1)
    if fmt == "e4m3":
        byte = np.frexp(amax)[1] - 1 + 127 - 7
    else:
        mant, ex = np.frexp(amax / 6.0)
        byte = np.where(mant > 0.5, ex, ex - 1) + 127
    byte = np.clip(np.where(amax > 0, byte, 1), 1, 254)
    scaled = (w * np.exp2(127.0 - byte)[:, None, :]).reshape(k, n).astype(np.float32)
    by_word = np.ascontiguousarray(scaled.reshape(k // 512, 128, 4, n).transpose(0, 1, 3, 2))
    if fmt == "e4m3":
        words = by_word.astype(ml_dtypes.float8_e4m3fn).view(np.uint8)
    else:
        c = by_word.astype(ml_dtypes.float4_e2m1fn).view(np.uint8) & 0xF
        words = c[..., 0::2] | (c[..., 1::2] << 4)
    return np.ascontiguousarray(words), np.ascontiguousarray(byte.astype(np.uint8).reshape(k // 512, 16, n))


def unpack_weight(words, scales, fmt):
    g, p, n, _ = words.shape
    if fmt == "e4m3":
        vals = np.ascontiguousarray(words).view(ml_dtypes.float8_e4m3fn).astype(np.float64)
    else:
        nib = np.empty((g, p, n, 4), np.uint8)
        nib[..., 0::2] = words & 0xF
        nib[..., 1::2] = words >> 4
        vals = E2M1[nib]
    vals = vals * np.repeat(np.exp2(scales.astype(np.float64) - 127.0), 8, axis=1)[..., None]
    return vals.transpose(0, 1, 3, 2).reshape(g * 512, n)
def pack4(w):
    words, scales = pack_weight(w, "e2m1")
    return words.reshape(words.shape[0], 128, -1), scales


def unpack4(words, scales):
    return unpack_weight(words.reshape(words.shape[0], 128, -1, 2), scales, "e2m1")


def planes(Y):
    n, m = Y.shape
    b = f64(bf(Y)).reshape(n // 32, 32, m)
    amax = np.abs(b).max(1)
    byte = np.clip(np.where(amax > 0, np.frexp(amax)[1] - 1 + 127 - 7, 1), 1, 254)
    codes = (b * np.exp2(127.0 - byte)[:, None, :]).reshape(n, m).astype(np.float32).astype(ml_dtypes.float8_e4m3fn).view(np.uint8)
    words = codes.reshape(n // 512, 128, 4, m).transpose(0, 1, 3, 2)
    return np.ascontiguousarray(words), np.ascontiguousarray(byte.astype(np.uint8).reshape(n // 512, 16, m))


S, K, G, M, R = 2048, 1024, 1024, 512, 512

def setup_inputs():
    s, u, t = mx_kscale(K), mx_kscale(M), mx_kscale(S)
    freq = np.random.uniform(0.2, 0.5, (K, 1))
    x = (np.random.binomial(2, freq, (K, S)) - 2 * freq) / np.sqrt(2 * freq * (1 - freq))
    geno_words, geno_scales = pack4(x / s[:, None])
    w = np.random.randn(K, G) * np.exp(0.5 * np.random.randn(G)) / np.sqrt(K)
    meas_words, meas_scales = pack_weight(np.random.randn(M, S) / u[:, None], "e4m3")
    return {
        "geno_words": geno_words, "geno_scales": geno_scales,
        "expr_w": bf(w * s[:, None]),
        "gene_scale": bf(1 / np.sqrt((w ** 2).sum(0))),
        "pred_weight": bf(np.exp(0.3 * np.random.randn(S)) * S ** -0.25 * t),
        "meas_words": meas_words, "meas_scales": meas_scales,
        "loadings": bf(np.random.randn(M, R) / np.sqrt(M) * u[:, None]),
        "offset": bf(0.4 * np.random.randn(R)),
        "trait_weight": bf(np.exp(0.3 * np.random.randn(S)) * S ** -0.25 / t),
        "earlier": bf(np.random.randn(G, R)),
        "gene_gain": bf(np.exp(0.8 * np.random.randn(G))),
    }

def reference(geno_words, geno_scales, expr_w, gene_scale, pred_weight, meas_words, meas_scales,
              loadings, offset, trait_weight, earlier, gene_gain):
    X = unpack4(geno_words, geno_scales)
    P = unpack_weight(meas_words, meas_scales, "e4m3")
    E = X.T @ mxq(f64(expr_w), 0)
    A = E * f64(gene_scale)[None, :] * f64(pred_weight)[:, None]
    T = P.T @ mxq(f64(loadings), 0)
    B = (T + f64(offset)[None, :]) * f64(trait_weight)[:, None]
    Z = mxq(A, 0).T @ mxq(B, 0)
    y = (Z + f64(earlier)) * f64(gene_gain)[:, None]
    Y = y.reshape(G, R)
    words, scales = planes(Y)
    return y, words, scales

@@ -1,0 +1,344 @@
+from contextlib import ExitStack
+
+import concourse.mybir as mybir
+from concourse.masks import make_identity
+
+S, K, G, M, R = 2048, 1024, 1024, 512, 512
+FLOPS = 2 * (S * K * G + S * M * R + G * R * S)
+
+F32 = mybir.dt.float32
+BF16 = mybir.dt.bfloat16
+I32 = mybir.dt.int32
+U32 = mybir.dt.uint32
+U8 = mybir.dt.uint8
+FP8X4 = mybir.dt.float8_e4m3fn_x4
+FP4X4 = mybir.dt.float4_e2m1fn_x4
+ALU = mybir.AluOpType
+ACT = mybir.ActivationFunctionType
+
+P = 128
+N = 512
+B_STEPS = 4
+A_STEPS = 8
+
+
+def tile_transcriptome_association_scores_k4_kernel(
+    tc, geno_words, geno_scales, expr_w, gene_scale, pred_weight, meas_words, meas_scales,
+    loadings, offset, trait_weight, earlier, gene_gain, out_0, out_1, out_2,
+):
+    nc = tc.nc
+    with ExitStack() as ctx:
+        keep = ctx.enter_context(tc.tile_pool(name="keep", bufs=1))
+        ring = ctx.enter_context(tc.tile_pool(name="ring", bufs=1))
+        psum = ctx.enter_context(tc.psum_pool(name="psum", bufs=1))
+        ctx.enter_context(tc.manual_schedule())
+
+        def kt(name, shape, dtype):
+            return keep.tile(shape, dtype, name=name, align_bytes=64)
+
+        def rt(tag, shape, dtype, bufs):
+            return ring.tile(shape, dtype, name=tag, tag=tag, bufs=bufs, align_bytes=64)
+
+        def bank(tag, shape, bufs):
+            return psum.tile(shape, F32, name=tag, tag=tag, bufs=bufs)
+
+        p_scales = kt("p_scales", [P, S], U8)
+        x_scales = kt("x_scales", [P, 2, S], U8)
+        nc.vector.memset(p_scales[:].bitcast(I32), 0)
+        nc.vector.memset(x_scales[:].rearrange("p k n -> p (k n)").bitcast(I32), 0)
+
+        tw_rows = kt("tw_rows", [P, 16], BF16)
+        pw_rows = kt("pw_rows", [P, 16], BF16)
+        l_raw = kt("l_raw", [P, 4, R], BF16)
+        nc.sync.dma_start(out=tw_rows[:], in_=trait_weight.rearrange("(p m) -> p m", m=16))
+        nc.sync.dma_start(out=l_raw[:], in_=loadings.rearrange("(p t) c -> p t c", t=4))
+        for q in range(4):
+            nc.scalar.dma_start(
+                out=p_scales[32 * q : 32 * q + 4, :].bitcast(I32),
+                in_=meas_scales[0, 4 * q : 4 * q + 4, :].bitcast(I32),
+            )
+        p_flat = meas_words[0].rearrange("p n t -> p (n t)")
+        p_first = kt("p_first", [P, N], U32)
+        p_rest = kt("p_rest", [P, 3 * N], U32)
+        nc.sync.dma_start(out=p_first[:].bitcast(I32), in_=p_flat[:, 0 : 4 * N].bitcast(I32))
+
+        off_col = kt("off_col", [P, 2, 2], BF16)
+        gs_col = kt("gs_col", [P, 2, 4], BF16)
+        gain_raw = kt("gain_raw", [P, 2, 4], BF16)
+        nc.sync.dma_start(out=off_col[:], in_=offset.rearrange("(h p j) -> p h j", h=2, j=2))
+        ident = kt("ident", [P, P], F32)
+        make_identity(nc, ident[:])
+        nc.sync.dma_start(out=p_rest[:].bitcast(I32), in_=p_flat[:, 4 * N :].bitcast(I32))
+        nc.sync.dma_start(out=pw_rows[:], in_=pred_weight.rearrange("(p m) -> p m", m=16))
+        nc.sync.dma_start(out=gs_col[:], in_=gene_scale.rearrange("(h p t) -> p h t", h=2, t=4))
+        nc.sync.dma_start(out=gain_raw[:], in_=gene_gain.rearrange("(h p t) -> p h t", h=2, t=4))
+
+        w_raw = []
+        for h in range(2):
+            w_half = kt("w_raw%d" % h, [P, 2, 4, N], BF16)
+            w_raw.append(w_half)
+
+        def load_w(h):
+            for k in range(2):
+                nc.sync.dma_start(
+                    out=w_raw[h][:, k, :, :],
+                    in_=expr_w[512 * k : 512 * k + 512, N * h : N * h + N].rearrange("(p t) c -> p t c", t=4),
+                )
+
+        load_w(0)
+        for q in range(4):
+            nc.sync.dma_start(
+                out=x_scales[32 * q : 32 * q + 4, :, :].bitcast(I32),
+                in_=geno_scales[:, 4 * q : 4 * q + 4, :].rearrange("k r n -> r k n").bitcast(I32),
+            )
+        x_words = []
+        for c in range(2):
+            x_half = kt("x_words%d" % c, [P, 2, 2048], U8)
+            nc.sync.dma_start(
+                out=x_half[:].bitcast(I32),
+                in_=geno_words[:, :, 2048 * c : 2048 * c + 2048].rearrange("k p b -> p k b").bitcast(I32),
+            )
+            x_words.append(x_half)
+        load_w(1)
+        e_raw = []
+        for h in range(2):
+            e_half = kt("e_raw%d" % h, [P, 4, R], BF16)
+            nc.sync.dma_start(out=e_half[:], in_=earlier[512 * h : 512 * h + 512, :].rearrange("(p t) r -> p t r", t=4))
+            e_raw.append(e_half)
+
+        def spread(rows, name, tag):
+            wide = kt(name, [P, S], BF16)
+            words = rows[:].bitcast(F32)
+            wide_words = wide[:].bitcast(F32).rearrange("p (n m) -> p n m", m=8)
+            for half in range(2):
+                ps = bank(tag, [P, 4, P], 2)
+                for m in range(4):
+                    col = 4 * half + m
+                    nc.tensor.transpose(ps[:, m, :], words[:, col : col + 1].to_broadcast([P, P]), ident[:])
+                nc.scalar.copy(out=wide_words[:, :, 4 * half : 4 * half + 4], in_=ps[:].rearrange("p m n -> p n m"))
+            return wide
+
+        tw_wide = spread(tw_rows, "tw_wide", "tr")
+        wides = {"tw": tw_wide}
+        gain_col = kt("gain_col", [P, 2, 4], F32)
+
+        l_grouped, l_codes, l_scales = [], [], []
+        for j in range(4):
+            lg = kt("l_grouped%d" % j, [P, P, 4], BF16)
+            lc = kt("l_codes%d" % j, [P, P], U32)
+            ls = kt("l_scales%d" % j, [P, P], U8)
+            l_grouped.append(lg)
+            l_codes.append(lc)
+            l_scales.append(ls)
+
+        def l_copy(j):
+            h, jj = divmod(j, 2)
+            src = l_raw[:, :, 256 * h : 256 * h + 256].rearrange("p t (m j) -> p j m t", j=2)
+            nc.vector.tensor_copy(out=l_grouped[j][:], in_=src[:, jj, :, :])
+
+        def quantize(codes, scales, src):
+            nc.vector.quantize_mx(out=codes.bitcast(FP8X4), scales=scales, in_=src)
+
+        def l_quant(j):
+            quantize(l_codes[j][:], l_scales[j][:], l_grouped[j][:].rearrange("p m t -> p (m t)"))
+
+        l_copy(0)
+        l_copy(1)
+        l_quant(0)
+        l_quant(1)
+        l_copy(2)
+        l_copy(3)
+        l_quant(2)
+        l_quant(3)
+
+        w_grouped, w_codes, w_scales = {}, {}, {}
+        staged, grouped, codes, scales = {}, {}, {}, {}
+        eg, zbank = {}, {}
+        y, y_grouped, y_codes, y_scales = [], [], [], []
+        for h in range(2):
+            yt = kt("y%d" % h, [P, 4, R], F32)
+            yg = kt("y_grouped%d" % h, [P, R, 4], BF16)
+            yc = kt("y_codes%d" % h, [P, R], U32)
+            ys = kt("y_scales%d" % h, [P, R], U8)
+            y.append(yt)
+            y_grouped.append(yg)
+            y_codes.append(yc)
+            y_scales.append(ys)
+
+        def w_copy(i):
+            h, t = divmod(i, 4)
+            wg = rt("w_grouped", [P, 2, P, 4], BF16, 3)
+            src = w_raw[h][:].rearrange("p k j (m t) -> p t k m j", t=4)
+            nc.scalar.copy(out=wg[:], in_=src[:, t, :, :, :])
+            w_grouped[i] = wg
+
+        def w_quant(i):
+            wc = rt("w_codes", [P, 2 * P], U32, 3)
+            ws = rt("w_scales", [P, 2 * P], U8, 3)
+            quantize(wc[:], ws[:], w_grouped[i][:].rearrange("p k m j -> p (k m j)"))
+            w_codes[i], w_scales[i] = wc, ws
+
+        def unit(s, u):
+            ps = bank("mm", [P, N], 4)
+            st = rt("staged", [P, N], BF16, 10)
+            staged[s, u] = st
+            if s < B_STEPS:
+                g = s
+                rhs = p_first[:] if g == 0 else p_rest[:, N * (g - 1) : N * g]
+                nc.tensor.matmul_mx(
+                    out=ps[:], lhsT=l_codes[u][:].bitcast(FP8X4), lhsT_scale=l_scales[u][:],
+                    rhs=rhs.bitcast(FP8X4), rhs_scale=p_scales[:, N * g : N * g + N], start=True, stop=True,
+                )
+                col, op0, wide = off_col[:, u // 2, u % 2 : u % 2 + 1], ALU.add, tw_wide
+            else:
+                i, g = s - B_STEPS, u
+                for k in range(2):
+                    rhs = x_words[g // 2][:, k, 1024 * (g % 2) : 1024 * (g % 2) + 1024]
+                    nc.tensor.matmul_mx(
+                        out=ps[:], lhsT=w_codes[i][:, P * k : P * k + P].bitcast(FP8X4),
+                        lhsT_scale=w_scales[i][:, P * k : P * k + P],
+                        rhs=rhs.bitcast(FP4X4), rhs_scale=x_scales[:, k, N * g : N * g + N],
+                        start=(k == 0), stop=(k == 1),
+                    )
+                col, op0, wide = gs_col[:, i // 4, i % 4 : i % 4 + 1], ALU.mult, wides["pw"]
+            nc.vector.scalar_tensor_tensor(
+                out=st[:].rearrange("p (u w) -> p u w", u=2),
+                in0=ps[:].rearrange("p (w u) -> p u w", u=2),
+                scalar=col,
+                in1=wide[:, N * g : N * g + N].rearrange("p (w u) -> p u w", u=2),
+                op0=op0, op1=ALU.mult,
+            )
+
+        def turn(s):
+            gr = rt("grouped", [P, 4 * N], BF16, 3)
+            grouped[s] = gr
+            gr_words = gr[:].bitcast(F32).rearrange("p (c m u) -> p c m u", c=4, u=2)
+            for half in range(2):
+                ps = bank("tr", [P, 2, 2, P], 2)
+                for cc in range(2):
+                    words = staged[s, 2 * half + cc][:].bitcast(F32)
+                    for u in range(2):
+                        nc.tensor.transpose(ps[:, cc, u, :], words[:, P * u : P * u + P], ident[:])
+                nc.scalar.copy(out=gr_words[:, 2 * half : 2 * half + 2, :, :], in_=ps[:].rearrange("p c u m -> p c m u"))
+
+        def step_quant(s, parts):
+            if s < B_STEPS:
+                cd = kt("b_codes%d" % s, [P, N], U32)
+                sc = kt("b_scales%d" % s, [P, N], U8)
+            else:
+                cd = rt("a_codes", [P, N], U32, 3)
+                sc = rt("a_scales", [P, N], U8, 3)
+            codes[s], scales[s] = cd, sc
+            w = N // parts
+            for part in range(parts):
+                quantize(cd[:, w * part : w * part + w], sc[:, w * part : w * part + w],
+                         grouped[s][:, 4 * w * part : 4 * w * part + 4 * w])
+
+        def z_passes(i, out, c0, c1):
+            s = i + B_STEPS
+            for g in range(4):
+                nc.tensor.matmul_mx(
+                    out=out, lhsT=codes[s][:, P * g : P * g + P].bitcast(FP8X4),
+                    lhsT_scale=scales[s][:, P * g : P * g + P],
+                    rhs=codes[g][:, c0:c1].bitcast(FP8X4), rhs_scale=scales[g][:, c0:c1],
+                    start=(g == 0), stop=(g == 3),
+                )
+
+        def z_whole(i):
+            ps = bank("z", [P, N], 2)
+            zbank[i] = ps
+            z_passes(i, ps[:], 0, N)
+
+        def make_eg(i):
+            h, t = divmod(i, 4)
+            e = rt("eg", [P, R], F32, 4)
+            eg[i] = e
+            nc.scalar.activation(out=e[:], in_=e_raw[h][:, t, :], func=ACT.Copy, scale=gain_col[:, h, t : t + 1])
+
+        def z_out(i, ps_half, half):
+            h, t = divmod(i, 4)
+            cols = slice(256 * half, 256 * half + 256)
+            nc.vector.scalar_tensor_tensor(
+                out=y[h][:, t, cols].rearrange("p (m j) -> p m j", j=2),
+                in0=ps_half.rearrange("p (j m) -> p m j", j=2),
+                scalar=gain_col[:, h, t : t + 1],
+                in1=eg[i][:, cols].rearrange("p (m j) -> p m j", j=2),
+                op0=ALU.mult, op1=ALU.add,
+            )
+
+        def store_y(i, c0, c1):
+            h, t = divmod(i, 4)
+            rows = out_0[512 * h : 512 * h + 512, :].rearrange("(p t) r -> p t r", t=4)
+            nc.sync.dma_start(out=rows[:, t, c0:c1], in_=y[h][:, t, c0:c1])
+
+        def y_copy(engine_copy, h, c0, c1):
+            engine_copy(out=y_grouped[h][:, c0:c1, :], in_=y[h][:, :, c0:c1].rearrange("p t r -> p r t"))
+
+        def y_quant(h, c0, c1):
+            quantize(y_codes[h][:, c0:c1], y_scales[h][:, c0:c1],
+                     y_grouped[h][:, c0:c1, :].rearrange("p r t -> p (r t)"))
+
+        def store_words(h, c0, c1):
+            dst = out_1[h].rearrange("p m t -> p (m t)")
+            nc.sync.dma_start(out=dst[:, 4 * c0 : 4 * c1].bitcast(I32), in_=y_codes[h][:, c0:c1].bitcast(I32))
+
+        def store_scales(h, queues):
+            for q in range(4):
+                queues[q].dma_start(
+                    out=out_2[h, 4 * q : 4 * q + 4, :].bitcast(I32),
+                    in_=y_scales[h][32 * q : 32 * q + 4, :].bitcast(I32),
+                )
+
+        steps = B_STEPS + A_STEPS
+        last = A_STEPS - 1
+        for tick in range(steps + 2):
+            if 0 <= tick - 2 < steps - 1:
+                step_quant(tick - 2, 1)
+            if tick - 2 == steps - 1:
+                step_quant(tick - 2, 2)
+            i_out = tick - 3 - B_STEPS
+            if 0 <= i_out < last:
+                for half in range(2):
+                    z_out(i_out, zbank[i_out][:, 256 * half : 256 * half + 256], half)
+                store_y(i_out, 0, R)
+            if tick < steps:
+                unit(tick, 0)
+                unit(tick, 1)
+            if 0 <= tick - 3 < A_STEPS:
+                w_quant(tick - 3)
+            if tick < steps:
+                unit(tick, 2)
+                unit(tick, 3)
+            if tick == 12:
+                y_quant(0, 0, R)
+                store_words(0, 0, R)
+                store_scales(0, [nc.sync] * 4)
+            if 0 <= tick - 1 < steps:
+                turn(tick - 1)
+            if tick == 1:
+                wides["pw"] = spread(pw_rows, "pw_wide", "z")
+                nc.scalar.activation(out=gain_col[:], in_=gain_raw[:], func=ACT.Copy)
+            if 0 <= tick - 2 < A_STEPS:
+                w_copy(tick - 2)
+            if 0 <= tick - 5 < A_STEPS:
+                make_eg(tick - 5)
+            if tick in (10, 11):
+                y_copy(nc.scalar.copy, 0, 256 * (tick - 10), 256 * (tick - 10) + 256)
+            i_z = tick - 2 - B_STEPS
+            if 0 <= i_z < last:
+                z_whole(i_z)
+
+        halves = []
+        for half in range(2):
+            ps = bank("mm", [P, N], 4)
+            z_passes(last, ps[:, 0:256], 256 * half, 256 * half + 256)
+            halves.append(ps)
+        z_out(last, halves[0][:, 0:256], 0)
+        y_copy(nc.scalar.copy, 1, 0, 256)
+        z_out(last, halves[1][:, 0:256], 1)
+        store_y(last, 0, R)
+        y_copy(nc.vector.tensor_copy, 1, 256, R)
+        y_quant(1, 0, 256)
+        y_quant(1, 256, R)
+        store_words(1, 0, R)
+        store_scales(1, [nc.scalar, nc.sync, nc.scalar, nc.sync])

@@ -18,6 +18,7 @@ ACT = mybir.ActivationFunctionType
 
 P = 128
 N = 512
+MMB, TRB, ZB = 4, 2, 2
 B_STEPS = 4
 A_STEPS = 8
 
@@ -49,76 +50,98 @@ def tile_transcriptome_association_scores_k4_kernel(
 
         tw_rows = kt("tw_rows", [P, 16], BF16)
         pw_rows = kt("pw_rows", [P, 16], BF16)
-        l_raw = kt("l_raw", [P, 4, R], BF16)
+        off_col = kt("off_col", [P, 2, 2], BF16)
+        gs_col = kt("gs_col", [P, 2, 4], BF16)
+        gain_raw = kt("gain_raw", [P, 2, 4], BF16)
+        l_raw, w_raw, x_words, e_raw, p_words = [], [], [], [], []
+        for h in range(2):
+            l_half = kt("l_raw%d" % h, [P, 4, 256], BF16)
+            w_half = kt("w_raw%d" % h, [P, 2, 4, N], BF16)
+            x_half = kt("x_words%d" % h, [P, 2, 2048], U8)
+            e_half = kt("e_raw%d" % h, [P, 4, R], BF16)
+            l_raw.append(l_half)
+            w_raw.append(w_half)
+            x_words.append(x_half)
+            e_raw.append(e_half)
+        for g in range(4):
+            p_part = kt("p_words%d" % g, [P, N], U32)
+            p_words.append(p_part)
+
+        def load_l(h):
+            rows = loadings.rearrange("(p t) c -> p t c", t=4)
+            nc.sync.dma_start(out=l_raw[h][:], in_=rows[:, :, 256 * h : 256 * h + 256])
+
+        def load_p(g):
+            flat = meas_words[0].rearrange("p n t -> p (n t)")
+            nc.sync.dma_start(out=p_words[g][:].bitcast(I32), in_=flat[:, 4 * N * g : 4 * N * g + 4 * N].bitcast(I32))
+
+        def load_w(h, k):
+            nc.sync.dma_start(
+                out=w_raw[h][:, k, :, :],
+                in_=expr_w[512 * k : 512 * k + 512, N * h : N * h + N].rearrange("(p t) c -> p t c", t=4),
+            )
+
+        def load_x(c):
+            nc.sync.dma_start(
+                out=x_words[c][:].bitcast(I32),
+                in_=geno_words[:, :, 2048 * c : 2048 * c + 2048].rearrange("k p b -> p k b").bitcast(I32),
+            )
+
+        def load_e(h):
+            nc.sync.dma_start(out=e_raw[h][:], in_=earlier[512 * h : 512 * h + 512, :].rearrange("(p t) r -> p t r", t=4))
+
         nc.sync.dma_start(out=tw_rows[:], in_=trait_weight.rearrange("(p m) -> p m", m=16))
-        nc.sync.dma_start(out=l_raw[:], in_=loadings.rearrange("(p t) c -> p t c", t=4))
+        l_all = kt("l_all", [P, 4, R], BF16)
+        nc.sync.dma_start(out=l_all[:], in_=loadings.rearrange("(p t) c -> p t c", t=4))
         for q in range(4):
             nc.scalar.dma_start(
                 out=p_scales[32 * q : 32 * q + 4, :].bitcast(I32),
                 in_=meas_scales[0, 4 * q : 4 * q + 4, :].bitcast(I32),
             )
-        p_flat = meas_words[0].rearrange("p n t -> p (n t)")
-        p_first = kt("p_first", [P, N], U32)
-        p_rest = kt("p_rest", [P, 3 * N], U32)
-        nc.sync.dma_start(out=p_first[:].bitcast(I32), in_=p_flat[:, 0 : 4 * N].bitcast(I32))
-
-        off_col = kt("off_col", [P, 2, 2], BF16)
-        gs_col = kt("gs_col", [P, 2, 4], BF16)
-        gain_raw = kt("gain_raw", [P, 2, 4], BF16)
+        load_p(0)
         nc.sync.dma_start(out=off_col[:], in_=offset.rearrange("(h p j) -> p h j", h=2, j=2))
         ident = kt("ident", [P, P], F32)
         make_identity(nc, ident[:])
-        nc.sync.dma_start(out=p_rest[:].bitcast(I32), in_=p_flat[:, 4 * N :].bitcast(I32))
         nc.sync.dma_start(out=pw_rows[:], in_=pred_weight.rearrange("(p m) -> p m", m=16))
-        nc.sync.dma_start(out=gs_col[:], in_=gene_scale.rearrange("(h p t) -> p h t", h=2, t=4))
-        nc.sync.dma_start(out=gain_raw[:], in_=gene_gain.rearrange("(h p t) -> p h t", h=2, t=4))
-
-        w_raw = []
-        for h in range(2):
-            w_half = kt("w_raw%d" % h, [P, 2, 4, N], BF16)
-            w_raw.append(w_half)
-
-        def load_w(h):
-            for k in range(2):
-                nc.sync.dma_start(
-                    out=w_raw[h][:, k, :, :],
-                    in_=expr_w[512 * k : 512 * k + 512, N * h : N * h + N].rearrange("(p t) c -> p t c", t=4),
-                )
-
-        load_w(0)
+        load_p(1)
+        load_w(0, 0)
+        load_w(0, 1)
+        load_p(2)
+        load_p(3)
         for q in range(4):
             nc.sync.dma_start(
                 out=x_scales[32 * q : 32 * q + 4, :, :].bitcast(I32),
                 in_=geno_scales[:, 4 * q : 4 * q + 4, :].rearrange("k r n -> r k n").bitcast(I32),
             )
-        x_words = []
-        for c in range(2):
-            x_half = kt("x_words%d" % c, [P, 2, 2048], U8)
-            nc.sync.dma_start(
-                out=x_half[:].bitcast(I32),
-                in_=geno_words[:, :, 2048 * c : 2048 * c + 2048].rearrange("k p b -> p k b").bitcast(I32),
-            )
-            x_words.append(x_half)
-        load_w(1)
-        e_raw = []
-        for h in range(2):
-            e_half = kt("e_raw%d" % h, [P, 4, R], BF16)
-            nc.sync.dma_start(out=e_half[:], in_=earlier[512 * h : 512 * h + 512, :].rearrange("(p t) r -> p t r", t=4))
-            e_raw.append(e_half)
+        load_x(0)
+        nc.sync.dma_start(out=gs_col[:], in_=gene_scale.rearrange("(h p t) -> p h t", h=2, t=4))
+        load_x(1)
+        load_w(1, 0)
+        load_w(1, 1)
+        nc.sync.dma_start(out=gain_raw[:], in_=gene_gain.rearrange("(h p t) -> p h t", h=2, t=4))
+        load_e(0)
+        load_e(1)
 
-        def spread(rows, name, tag):
+        def spread(rows, name, tag, cuts):
+            by_parity = kt(name + "_rows", [P, 2, 8], BF16)
+            nc.scalar.activation(out=by_parity[:], in_=rows[:].rearrange("p (w u) -> p u w", u=2), func=ACT.Identity)
+            words = by_parity[:].rearrange("p u w -> p (u w)").bitcast(F32)
             wide = kt(name, [P, S], BF16)
-            words = rows[:].bitcast(F32)
-            wide_words = wide[:].bitcast(F32).rearrange("p (n m) -> p n m", m=8)
-            for half in range(2):
-                ps = bank(tag, [P, 4, P], 2)
-                for m in range(4):
-                    col = 4 * half + m
-                    nc.tensor.transpose(ps[:, m, :], words[:, col : col + 1].to_broadcast([P, P]), ident[:])
-                nc.scalar.copy(out=wide_words[:, :, 4 * half : 4 * half + 4], in_=ps[:].rearrange("p m n -> p n m"))
+            wide_words = wide[:].bitcast(F32).rearrange("p (g u n c) -> p u g n c", g=4, u=2, c=4)
+            banks = []
+            for u in range(2):
+                ps = bank(tag, [P, 4, P], TRB if tag == "tr" else ZB)
+                banks.append(ps)
+                for c in range(4):
+                    col = 4 * u + c
+                    nc.tensor.transpose(ps[:, c, :], words[:, col : col + 1].to_broadcast([P, P]), ident[:])
+            for g0, g1 in cuts:
+                for u in range(2):
+                    nc.scalar.copy(out=wide_words[:, u, g0:g1, :, :],
+                                   in_=banks[u][:].rearrange("p c (g n) -> p g n c", g=4)[:, g0:g1, :, :])
             return wide
 
-        tw_wide = spread(tw_rows, "tw_wide", "tr")
+        tw_wide = spread(tw_rows, "tw_wide", "tr", [(0, 1), (1, 4)])
         wides = {"tw": tw_wide}
         gain_col = kt("gain_col", [P, 2, 4], F32)
 
@@ -131,10 +154,10 @@ def tile_transcriptome_association_scores_k4_kernel(
             l_codes.append(lc)
             l_scales.append(ls)
 
-        def l_copy(j):
+        def l_copy(engine_copy, j):
             h, jj = divmod(j, 2)
-            src = l_raw[:, :, 256 * h : 256 * h + 256].rearrange("p t (m j) -> p j m t", j=2)
-            nc.vector.tensor_copy(out=l_grouped[j][:], in_=src[:, jj, :, :])
+            src = l_all[:, :, 256 * h : 256 * h + 256].rearrange("p t (m j) -> p j m t", j=2)
+            engine_copy(out=l_grouped[j][:], in_=src[:, jj, :, :])
 
         def quantize(codes, scales, src):
             nc.vector.quantize_mx(out=codes.bitcast(FP8X4), scales=scales, in_=src)
@@ -142,18 +165,18 @@ def tile_transcriptome_association_scores_k4_kernel(
         def l_quant(j):
             quantize(l_codes[j][:], l_scales[j][:], l_grouped[j][:].rearrange("p m t -> p (m t)"))
 
-        l_copy(0)
-        l_copy(1)
+        l_copy(nc.vector.tensor_copy, 0)
+        l_copy(nc.vector.tensor_copy, 1)
         l_quant(0)
         l_quant(1)
-        l_copy(2)
-        l_copy(3)
+        l_copy(nc.vector.tensor_copy, 2)
+        l_copy(nc.vector.tensor_copy, 3)
         l_quant(2)
         l_quant(3)
 
         w_grouped, w_codes, w_scales = {}, {}, {}
         staged, grouped, codes, scales = {}, {}, {}, {}
-        eg, zbank = {}, {}
+        eg, zbank, mm_bank = {}, {}, {}
         y, y_grouped, y_codes, y_scales = [], [], [], []
         for h in range(2):
             yt = kt("y%d" % h, [P, 4, R], F32)
@@ -165,31 +188,28 @@ def tile_transcriptome_association_scores_k4_kernel(
             y_codes.append(yc)
             y_scales.append(ys)
 
-        def w_copy(i):
-            h, t = divmod(i, 4)
-            wg = rt("w_grouped", [P, 2, P, 4], BF16, 3)
-            src = w_raw[h][:].rearrange("p k j (m t) -> p t k m j", t=4)
-            nc.scalar.copy(out=wg[:], in_=src[:, t, :, :, :])
-            w_grouped[i] = wg
+        def w_copy(pair, k):
+            h, tt = divmod(pair, 2)
+            if k == 0:
+                w_grouped[pair] = rt("w_grouped", [P, 2, 2, P, 4], BF16, 2)
+            src = w_raw[h][:, k, :, :].rearrange("p j (m t) -> p m t j", t=4)
+            nc.scalar.copy(out=w_grouped[pair][:, :, k, :, :].rearrange("p t m j -> p m t j"),
+                           in_=src[:, :, 2 * tt : 2 * tt + 2, :])
 
         def w_quant(i):
             wc = rt("w_codes", [P, 2 * P], U32, 3)
             ws = rt("w_scales", [P, 2 * P], U8, 3)
-            quantize(wc[:], ws[:], w_grouped[i][:].rearrange("p k m j -> p (k m j)"))
+            quantize(wc[:], ws[:], w_grouped[i // 2][:, i % 2, :, :, :].rearrange("p k m j -> p (k m j)"))
             w_codes[i], w_scales[i] = wc, ws
 
-        def unit(s, u):
-            ps = bank("mm", [P, N], 4)
-            st = rt("staged", [P, N], BF16, 10)
-            staged[s, u] = st
+        def product(s, u):
+            ps = bank("mm", [P, N], MMB)
+            mm_bank[s, u] = ps
             if s < B_STEPS:
-                g = s
-                rhs = p_first[:] if g == 0 else p_rest[:, N * (g - 1) : N * g]
                 nc.tensor.matmul_mx(
                     out=ps[:], lhsT=l_codes[u][:].bitcast(FP8X4), lhsT_scale=l_scales[u][:],
-                    rhs=rhs.bitcast(FP8X4), rhs_scale=p_scales[:, N * g : N * g + N], start=True, stop=True,
+                    rhs=p_words[s][:].bitcast(FP8X4), rhs_scale=p_scales[:, N * s : N * s + N], start=True, stop=True,
                 )
-                col, op0, wide = off_col[:, u // 2, u % 2 : u % 2 + 1], ALU.add, tw_wide
             else:
                 i, g = s - B_STEPS, u
                 for k in range(2):
@@ -200,21 +220,38 @@ def tile_transcriptome_association_scores_k4_kernel(
                         rhs=rhs.bitcast(FP4X4), rhs_scale=x_scales[:, k, N * g : N * g + N],
                         start=(k == 0), stop=(k == 1),
                     )
-                col, op0, wide = gs_col[:, i // 4, i % 4 : i % 4 + 1], ALU.mult, wides["pw"]
-            nc.vector.scalar_tensor_tensor(
-                out=st[:].rearrange("p (u w) -> p u w", u=2),
-                in0=ps[:].rearrange("p (w u) -> p u w", u=2),
-                scalar=col,
-                in1=wide[:, N * g : N * g + N].rearrange("p (w u) -> p u w", u=2),
-                op0=op0, op1=ALU.mult,
-            )
+
+        def weigh(s, u, on_pool=False):
+            st = rt("staged", [P, N], BF16, 12)
+            staged[s, u] = st
+            if s < B_STEPS:
+                g, col, op0, wide = s, off_col[:, u // 2, u % 2 : u % 2 + 1], ALU.add, tw_wide
+            else:
+                i = s - B_STEPS
+                g, col, op0, wide = u, gs_col[:, i // 4, i % 4 : i % 4 + 1], ALU.mult, wides["pw"]
+            by_parity = mm_bank[s, u][:].rearrange("p (w u) -> p u w", u=2)
+            if on_pool:
+                shifted = rt("shifted", [P, N], F32, 2)
+                nc.scalar.activation(out=shifted[:].rearrange("p (u w) -> p u w", u=2), in_=by_parity,
+                                     func=ACT.Identity, bias=col)
+                nc.gpsimd.tensor_tensor(out=st[:], in0=shifted[:], in1=wide[:, N * g : N * g + N], op=ALU.mult)
+            else:
+                nc.vector.scalar_tensor_tensor(
+                    out=st[:].rearrange("p (u w) -> p u w", u=2), in0=by_parity, scalar=col,
+                    in1=wide[:, N * g : N * g + N].rearrange("p (u w) -> p u w", u=2),
+                    op0=op0, op1=ALU.mult,
+                )
+
+        def unit(s, u):
+            product(s, u)
+            weigh(s, u)
 
         def turn(s):
-            gr = rt("grouped", [P, 4 * N], BF16, 3)
+            gr = rt("grouped", [P, 4 * N], BF16, 6)
             grouped[s] = gr
             gr_words = gr[:].bitcast(F32).rearrange("p (c m u) -> p c m u", c=4, u=2)
             for half in range(2):
-                ps = bank("tr", [P, 2, 2, P], 2)
+                ps = bank("tr", [P, 2, 2, P], TRB)
                 for cc in range(2):
                     words = staged[s, 2 * half + cc][:].bitcast(F32)
                     for u in range(2):
@@ -245,7 +282,7 @@ def tile_transcriptome_association_scores_k4_kernel(
                 )
 
         def z_whole(i):
-            ps = bank("z", [P, N], 2)
+            ps = bank("z", [P, N], ZB)
             zbank[i] = ps
             z_passes(i, ps[:], 0, N)
 
@@ -292,53 +329,66 @@ def tile_transcriptome_association_scores_k4_kernel(
         steps = B_STEPS + A_STEPS
         last = A_STEPS - 1
         for tick in range(steps + 2):
-            if 0 <= tick - 2 < steps - 1:
-                step_quant(tick - 2, 1)
+            i_out = tick - 3 - B_STEPS
+            early = tick <= 4
+            if early:
+                unit(tick, 0)
+            for sq in range(steps - 1):
+                if tick == ((4,5,6,6)[sq] if sq < B_STEPS else sq + 2):
+                    step_quant(sq, 1)
             if tick - 2 == steps - 1:
                 step_quant(tick - 2, 2)
-            i_out = tick - 3 - B_STEPS
+            if tick == 3:
+                w_quant(0)
             if 0 <= i_out < last:
                 for half in range(2):
                     z_out(i_out, zbank[i_out][:, 256 * half : 256 * half + 256], half)
                 store_y(i_out, 0, R)
+            if tick in (10, 11):
+                y_copy(nc.scalar.copy, 0, 256 * (tick - 10), 256 * (tick - 10) + 256)
             if tick < steps:
-                unit(tick, 0)
+                if not early:
+                    unit(tick, 0)
                 unit(tick, 1)
-            if 0 <= tick - 3 < A_STEPS:
-                w_quant(tick - 3)
-            if tick < steps:
+                if 1 <= tick - 3 < A_STEPS:
+                    w_quant(tick - 3)
                 unit(tick, 2)
                 unit(tick, 3)
-            if tick == 12:
+            if tick == 11:
                 y_quant(0, 0, R)
                 store_words(0, 0, R)
                 store_scales(0, [nc.sync] * 4)
             if 0 <= tick - 1 < steps:
                 turn(tick - 1)
-            if tick == 1:
-                wides["pw"] = spread(pw_rows, "pw_wide", "z")
+            if tick == 0:
+                wides["pw"] = spread(pw_rows, "pw_wide", "z", [(0, 4)])
+            if tick <= 1:
+                w_copy(0, tick)
+            if 3 <= tick <= 8:
+                w_copy((tick - 1) // 2, (tick - 1) % 2)
+            if tick == 4:
                 nc.scalar.activation(out=gain_col[:], in_=gain_raw[:], func=ACT.Copy)
-            if 0 <= tick - 2 < A_STEPS:
-                w_copy(tick - 2)
             if 0 <= tick - 5 < A_STEPS:
                 make_eg(tick - 5)
-            if tick in (10, 11):
-                y_copy(nc.scalar.copy, 0, 256 * (tick - 10), 256 * (tick - 10) + 256)
             i_z = tick - 2 - B_STEPS
             if 0 <= i_z < last:
                 z_whole(i_z)
 
         halves = []
         for half in range(2):
-            ps = bank("mm", [P, N], 4)
+            ps = bank("mm", [P, N], MMB)
             z_passes(last, ps[:, 0:256], 256 * half, 256 * half + 256)
             halves.append(ps)
         z_out(last, halves[0][:, 0:256], 0)
-        y_copy(nc.scalar.copy, 1, 0, 256)
+        store_y(last, 0, 256)
+        y_copy(nc.scalar.copy, 1, 0, 128)
+        y_copy(nc.vector.tensor_copy, 1, 128, 256)
         z_out(last, halves[1][:, 0:256], 1)
-        store_y(last, 0, R)
-        y_copy(nc.vector.tensor_copy, 1, 256, R)
+        store_y(last, 256, R)
+        y_copy(nc.scalar.copy, 1, 256, 384)
         y_quant(1, 0, 256)
+        store_words(1, 0, 256)
+        y_copy(nc.vector.tensor_copy, 1, 384, R)
         y_quant(1, 256, R)
-        store_words(1, 0, R)
+        store_words(1, 256, R)
         store_scales(1, [nc.scalar, nc.sync, nc.scalar, nc.sync])

@@ -3,8 +3,8 @@ from contextlib import ExitStack
 import concourse.mybir as mybir
 from concourse.masks import make_identity
 
-S, K, G, M, R = 2048, 1024, 1024, 512, 512
-FLOPS = 2 * (S * K * G + S * M * R + G * R * S)
+SAMPLES, VARIANTS, GENES, MEASURES, TRAITS = 2048, 1024, 1024, 512, 512
+FLOPS = 2 * (SAMPLES * VARIANTS * GENES + SAMPLES * MEASURES * TRAITS + GENES * TRAITS * SAMPLES)
 
 F32 = mybir.dt.float32
 BF16 = mybir.dt.bfloat16
@@ -17,10 +17,25 @@ ALU = mybir.AluOpType
 ACT = mybir.ActivationFunctionType
 
 P = 128
-N = 512
-MMB, TRB, ZB = 4, 2, 2
-B_STEPS = 4
-A_STEPS = 8
+PACK = 4
+GROUP = P * PACK
+SAMPLE_GROUPS = SAMPLES // GROUP
+VARIANT_GROUPS = VARIANTS // GROUP
+GENE_GROUPS = GENES // GROUP
+GENE_TILES = GENES // P
+TRAIT_TILES = TRAITS // P
+HALF = TRAITS // 2
+QUARTER = TRAITS // 4
+
+BANKS = 4
+B_STEPS = SAMPLE_GROUPS
+STEPS = B_STEPS + GENE_TILES
+
+TURN_LAG = 1
+SCORE_LAG = 2
+FINISH_LAG = 3
+FIRST_SCORE_TICK = B_STEPS + SCORE_LAG
+B_QUANTIZE_LAG = 4
 
 
 def tile_transcriptome_association_scores_k4_kernel(
@@ -34,79 +49,70 @@ def tile_transcriptome_association_scores_k4_kernel(
         psum = ctx.enter_context(tc.psum_pool(name="psum", bufs=1))
         ctx.enter_context(tc.manual_schedule())
 
-        def kt(name, shape, dtype):
+        def kept(name, shape, dtype):
             return keep.tile(shape, dtype, name=name, align_bytes=64)
 
-        def rt(tag, shape, dtype, bufs):
+        def kept_list(name, count, shape, dtype):
+            return [kept("%s%d" % (name, n), shape, dtype) for n in range(count)]
+
+        def rotating(tag, shape, dtype, bufs):
             return ring.tile(shape, dtype, name=tag, tag=tag, bufs=bufs, align_bytes=64)
 
-        def bank(tag, shape, bufs):
-            return psum.tile(shape, F32, name=tag, tag=tag, bufs=bufs)
+        psum_banks = {"product": BANKS, "turn": 2, "score": 2}
 
-        p_scales = kt("p_scales", [P, S], U8)
-        x_scales = kt("x_scales", [P, 2, S], U8)
+        def bank(tag, shape):
+            return psum.tile(shape, F32, name=tag, tag=tag, bufs=psum_banks[tag])
+
+        def quantize(codes, scales, values):
+            nc.vector.quantize_mx(out=codes.bitcast(FP8X4), scales=scales, in_=values)
+
+        p_scales = kept("p_scales", [P, SAMPLES], U8)
+        x_scales = kept("x_scales", [P, VARIANT_GROUPS, SAMPLES], U8)
         nc.vector.memset(p_scales[:].bitcast(I32), 0)
         nc.vector.memset(x_scales[:].rearrange("p k n -> p (k n)").bitcast(I32), 0)
 
-        tw_rows = kt("tw_rows", [P, 16], BF16)
-        pw_rows = kt("pw_rows", [P, 16], BF16)
-        off_col = kt("off_col", [P, 2, 2], BF16)
-        gs_col = kt("gs_col", [P, 2, 4], BF16)
-        gain_raw = kt("gain_raw", [P, 2, 4], BF16)
-        l_raw, w_raw, x_words, e_raw, p_words = [], [], [], [], []
-        for h in range(2):
-            l_half = kt("l_raw%d" % h, [P, 4, 256], BF16)
-            w_half = kt("w_raw%d" % h, [P, 2, 4, N], BF16)
-            x_half = kt("x_words%d" % h, [P, 2, 2048], U8)
-            e_half = kt("e_raw%d" % h, [P, 4, R], BF16)
-            l_raw.append(l_half)
-            w_raw.append(w_half)
-            x_words.append(x_half)
-            e_raw.append(e_half)
-        for g in range(4):
-            p_part = kt("p_words%d" % g, [P, N], U32)
-            p_words.append(p_part)
-
-        def load_l(h):
-            rows = loadings.rearrange("(p t) c -> p t c", t=4)
-            nc.sync.dma_start(out=l_raw[h][:], in_=rows[:, :, 256 * h : 256 * h + 256])
+        per_row = SAMPLES // P
+        trait_weight_rows = kept("trait_weight_rows", [P, per_row], BF16)
+        pred_weight_rows = kept("pred_weight_rows", [P, per_row], BF16)
+        offset_cols = kept("offset_cols", [P, 2, 2], BF16)
+        gene_scale_cols = kept("gene_scale_cols", [P, GENE_GROUPS, PACK], BF16)
+        gain_raw = kept("gain_raw", [P, GENE_GROUPS, PACK], BF16)
+        l_raw = kept("l_raw", [P, PACK, TRAITS], BF16)
+        w_raw = kept_list("w_raw", GENE_GROUPS, [P, VARIANT_GROUPS, PACK, GROUP], BF16)
+        p_words = kept_list("p_words", SAMPLE_GROUPS, [P, GROUP], U32)
+        x_words = kept_list("x_words", 2, [P, VARIANT_GROUPS, SAMPLES], U8)
+        earlier_raw = kept_list("earlier_raw", GENE_GROUPS, [P, PACK, TRAITS], BF16)
 
         def load_p(g):
             flat = meas_words[0].rearrange("p n t -> p (n t)")
-            nc.sync.dma_start(out=p_words[g][:].bitcast(I32), in_=flat[:, 4 * N * g : 4 * N * g + 4 * N].bitcast(I32))
+            src = flat[:, PACK * GROUP * g : PACK * GROUP * (g + 1)]
+            nc.sync.dma_start(out=p_words[g][:].bitcast(I32), in_=src.bitcast(I32))
 
         def load_w(h, k):
-            nc.sync.dma_start(
-                out=w_raw[h][:, k, :, :],
-                in_=expr_w[512 * k : 512 * k + 512, N * h : N * h + N].rearrange("(p t) c -> p t c", t=4),
-            )
+            src = expr_w[GROUP * k : GROUP * (k + 1), GROUP * h : GROUP * (h + 1)]
+            nc.sync.dma_start(out=w_raw[h][:, k, :, :], in_=src.rearrange("(p t) c -> p t c", t=PACK))
 
-        def load_x(c):
-            nc.sync.dma_start(
-                out=x_words[c][:].bitcast(I32),
-                in_=geno_words[:, :, 2048 * c : 2048 * c + 2048].rearrange("k p b -> p k b").bitcast(I32),
-            )
+        def load_x(half):
+            src = geno_words[:, :, SAMPLES * half : SAMPLES * (half + 1)]
+            nc.sync.dma_start(out=x_words[half][:].bitcast(I32), in_=src.rearrange("k p b -> p k b").bitcast(I32))
 
-        def load_e(h):
-            nc.sync.dma_start(out=e_raw[h][:], in_=earlier[512 * h : 512 * h + 512, :].rearrange("(p t) r -> p t r", t=4))
+        def load_gene_cols(cols, vector):
+            nc.sync.dma_start(out=cols[:], in_=vector.rearrange("(h p t) -> p h t", h=GENE_GROUPS, t=PACK))
 
-        nc.sync.dma_start(out=tw_rows[:], in_=trait_weight.rearrange("(p m) -> p m", m=16))
-        l_all = kt("l_all", [P, 4, R], BF16)
-        nc.sync.dma_start(out=l_all[:], in_=loadings.rearrange("(p t) c -> p t c", t=4))
+        nc.sync.dma_start(out=trait_weight_rows[:], in_=trait_weight.rearrange("(p m) -> p m", m=per_row))
+        nc.sync.dma_start(out=l_raw[:], in_=loadings.rearrange("(p t) c -> p t c", t=PACK))
         for q in range(4):
             nc.scalar.dma_start(
                 out=p_scales[32 * q : 32 * q + 4, :].bitcast(I32),
                 in_=meas_scales[0, 4 * q : 4 * q + 4, :].bitcast(I32),
             )
         load_p(0)
-        nc.sync.dma_start(out=off_col[:], in_=offset.rearrange("(h p j) -> p h j", h=2, j=2))
-        ident = kt("ident", [P, P], F32)
-        make_identity(nc, ident[:])
-        nc.sync.dma_start(out=pw_rows[:], in_=pred_weight.rearrange("(p m) -> p m", m=16))
+        nc.sync.dma_start(out=offset_cols[:], in_=offset.rearrange("(h p c) -> p h c", h=2, c=2))
+        nc.sync.dma_start(out=pred_weight_rows[:], in_=pred_weight.rearrange("(p m) -> p m", m=per_row))
         load_p(1)
         load_w(0, 0)
-        load_w(0, 1)
         load_p(2)
+        load_w(0, 1)
         load_p(3)
         for q in range(4):
             nc.sync.dma_start(
@@ -114,281 +120,250 @@ def tile_transcriptome_association_scores_k4_kernel(
                 in_=geno_scales[:, 4 * q : 4 * q + 4, :].rearrange("k r n -> r k n").bitcast(I32),
             )
         load_x(0)
-        nc.sync.dma_start(out=gs_col[:], in_=gene_scale.rearrange("(h p t) -> p h t", h=2, t=4))
+        load_gene_cols(gene_scale_cols, gene_scale)
         load_x(1)
         load_w(1, 0)
         load_w(1, 1)
-        nc.sync.dma_start(out=gain_raw[:], in_=gene_gain.rearrange("(h p t) -> p h t", h=2, t=4))
-        load_e(0)
-        load_e(1)
+        load_gene_cols(gain_raw, gene_gain)
+        for h in range(GENE_GROUPS):
+            src = earlier[GROUP * h : GROUP * (h + 1), :]
+            nc.sync.dma_start(out=earlier_raw[h][:], in_=src.rearrange("(p t) r -> p t r", t=PACK))
 
-        def spread(rows, name, tag, cuts):
-            by_parity = kt(name + "_rows", [P, 2, 8], BF16)
-            nc.scalar.activation(out=by_parity[:], in_=rows[:].rearrange("p (w u) -> p u w", u=2), func=ACT.Identity)
-            words = by_parity[:].rearrange("p u w -> p (u w)").bitcast(F32)
-            wide = kt(name, [P, S], BF16)
-            wide_words = wide[:].bitcast(F32).rearrange("p (g u n c) -> p u g n c", g=4, u=2, c=4)
+        ident = kept("ident", [P, P], F32)
+        make_identity(nc, ident[:])
+        warm = kept("warm", [P, 1], F32)
+        nc.scalar.activation(out=warm[:], in_=ident[:, 0:1], func=ACT.Copy)
+
+        def spread(rows, name, tag, sort_copy, group_ranges):
+            by_parity = kept(name + "_sorted", [P, 2, per_row // 2], BF16)
+            sort_copy(out=by_parity[:], in_=rows[:].rearrange("p (w u) -> p u w", u=2))
+            words = by_parity[:].bitcast(F32)
+            wide = kept(name, [P, SAMPLES], BF16)
+            wide_words = wide[:].bitcast(F32).rearrange("p (g u n c) -> p u g n c", g=SAMPLE_GROUPS, u=2, c=4)
             banks = []
             for u in range(2):
-                ps = bank(tag, [P, 4, P], TRB if tag == "tr" else ZB)
-                banks.append(ps)
+                spread_bank = bank(tag, [P, 4, P])
+                banks.append(spread_bank[:].rearrange("p c (g n) -> p g n c", g=SAMPLE_GROUPS))
                 for c in range(4):
-                    col = 4 * u + c
-                    nc.tensor.transpose(ps[:, c, :], words[:, col : col + 1].to_broadcast([P, P]), ident[:])
-            for g0, g1 in cuts:
+                    nc.tensor.transpose(spread_bank[:, c, :], words[:, u, c : c + 1].to_broadcast([P, P]), ident[:])
+            for g0, g1 in group_ranges:
                 for u in range(2):
-                    nc.scalar.copy(out=wide_words[:, u, g0:g1, :, :],
-                                   in_=banks[u][:].rearrange("p c (g n) -> p g n c", g=4)[:, g0:g1, :, :])
+                    nc.scalar.copy(out=wide_words[:, u, g0:g1, :, :], in_=banks[u][:, g0:g1, :, :])
             return wide
 
-        tw_wide = spread(tw_rows, "tw_wide", "tr", [(0, 1), (1, 4)])
-        wides = {"tw": tw_wide}
-        gain_col = kt("gain_col", [P, 2, 4], F32)
+        l_grouped = kept_list("l_grouped", TRAIT_TILES, [P, P, PACK], BF16)
+        l_codes = kept_list("l_codes", TRAIT_TILES, [P, P], U32)
+        l_scales = kept_list("l_scales", TRAIT_TILES, [P, P], U8)
 
-        l_grouped, l_codes, l_scales = [], [], []
-        for j in range(4):
-            lg = kt("l_grouped%d" % j, [P, P, 4], BF16)
-            lc = kt("l_codes%d" % j, [P, P], U32)
-            ls = kt("l_scales%d" % j, [P, P], U8)
-            l_grouped.append(lg)
-            l_codes.append(lc)
-            l_scales.append(ls)
+        def group_l(copy, j):
+            src = l_raw[:].rearrange("p t (h m c) -> p h c m t", h=2, c=2)
+            copy(out=l_grouped[j][:], in_=src[:, j // 2, j % 2, :, :])
 
-        def l_copy(engine_copy, j):
-            h, jj = divmod(j, 2)
-            src = l_all[:, :, 256 * h : 256 * h + 256].rearrange("p t (m j) -> p j m t", j=2)
-            engine_copy(out=l_grouped[j][:], in_=src[:, jj, :, :])
-
-        def quantize(codes, scales, src):
-            nc.vector.quantize_mx(out=codes.bitcast(FP8X4), scales=scales, in_=src)
-
-        def l_quant(j):
+        def quantize_l(j):
             quantize(l_codes[j][:], l_scales[j][:], l_grouped[j][:].rearrange("p m t -> p (m t)"))
 
-        l_copy(nc.vector.tensor_copy, 0)
-        l_copy(nc.vector.tensor_copy, 1)
-        l_quant(0)
-        l_quant(1)
-        l_copy(nc.vector.tensor_copy, 2)
-        l_copy(nc.vector.tensor_copy, 3)
-        l_quant(2)
-        l_quant(3)
+        group_l(nc.scalar.copy, 1)
+        sample_weights = {}
+        sample_weights["trait"] = spread(
+            trait_weight_rows, "trait_weight_wide", "turn", nc.vector.tensor_copy, [(0, 1), (1, SAMPLE_GROUPS)]
+        )
+        group_l(nc.vector.tensor_copy, 0)
+        quantize_l(0)
+        quantize_l(1)
+        group_l(nc.vector.tensor_copy, 2)
+        group_l(nc.vector.tensor_copy, 3)
+        quantize_l(2)
+        quantize_l(3)
 
+        gain_cols = kept("gain_cols", [P, GENE_GROUPS, PACK], F32)
+        y = kept_list("y", GENE_GROUPS, [P, PACK, TRAITS], F32)
+        y_grouped = kept_list("y_grouped", GENE_GROUPS, [P, TRAITS, PACK], BF16)
+        y_codes = kept_list("y_codes", GENE_GROUPS, [P, TRAITS], U32)
+        y_scales = kept_list("y_scales", GENE_GROUPS, [P, TRAITS], U8)
         w_grouped, w_codes, w_scales = {}, {}, {}
-        staged, grouped, codes, scales = {}, {}, {}, {}
-        eg, zbank, mm_bank = {}, {}, {}
-        y, y_grouped, y_codes, y_scales = [], [], [], []
-        for h in range(2):
-            yt = kt("y%d" % h, [P, 4, R], F32)
-            yg = kt("y_grouped%d" % h, [P, R, 4], BF16)
-            yc = kt("y_codes%d" % h, [P, R], U32)
-            ys = kt("y_scales%d" % h, [P, R], U8)
-            y.append(yt)
-            y_grouped.append(yg)
-            y_codes.append(yc)
-            y_scales.append(ys)
+        weighted, grouped, codes, scales = {}, {}, {}, {}
+        earlier_gained, score_banks = {}, {}
 
-        def w_copy(pair, k):
-            h, tt = divmod(pair, 2)
+        def group_w(pair, k):
+            h, first = pair // 2, 2 * (pair % 2)
             if k == 0:
-                w_grouped[pair] = rt("w_grouped", [P, 2, 2, P, 4], BF16, 2)
-            src = w_raw[h][:, k, :, :].rearrange("p j (m t) -> p m t j", t=4)
-            nc.scalar.copy(out=w_grouped[pair][:, :, k, :, :].rearrange("p t m j -> p m t j"),
-                           in_=src[:, :, 2 * tt : 2 * tt + 2, :])
+                w_grouped[pair] = rotating("w_grouped", [P, 2, VARIANT_GROUPS, P, PACK], BF16, 2)
+            src = w_raw[h][:, k, :, :].rearrange("p j (m t) -> p m t j", t=PACK)
+            dst = w_grouped[pair][:, :, k, :, :].rearrange("p t m j -> p m t j")
+            nc.scalar.copy(out=dst, in_=src[:, :, first : first + 2, :])
 
-        def w_quant(i):
-            wc = rt("w_codes", [P, 2 * P], U32, 3)
-            ws = rt("w_scales", [P, 2 * P], U8, 3)
-            quantize(wc[:], ws[:], w_grouped[i // 2][:, i % 2, :, :, :].rearrange("p k m j -> p (k m j)"))
-            w_codes[i], w_scales[i] = wc, ws
+        def quantize_w(i):
+            w_codes[i] = rotating("w_codes", [P, VARIANT_GROUPS * P], U32, 3)
+            w_scales[i] = rotating("w_scales", [P, VARIANT_GROUPS * P], U8, 3)
+            values = w_grouped[i // 2][:, i % 2, :, :, :].rearrange("p k m j -> p (k m j)")
+            quantize(w_codes[i][:], w_scales[i][:], values)
 
-        def product(s, u):
-            ps = bank("mm", [P, N], MMB)
-            mm_bank[s, u] = ps
-            if s < B_STEPS:
+        def product(step, b):
+            acc = bank("product", [P, GROUP])
+            if step < B_STEPS:
+                g = step
                 nc.tensor.matmul_mx(
-                    out=ps[:], lhsT=l_codes[u][:].bitcast(FP8X4), lhsT_scale=l_scales[u][:],
-                    rhs=p_words[s][:].bitcast(FP8X4), rhs_scale=p_scales[:, N * s : N * s + N], start=True, stop=True,
+                    out=acc[:], lhsT=l_codes[b][:].bitcast(FP8X4), lhsT_scale=l_scales[b][:],
+                    rhs=p_words[g][:].bitcast(FP8X4), rhs_scale=p_scales[:, GROUP * g : GROUP * (g + 1)],
+                    start=True, stop=True,
                 )
+                per_partition, first_op = offset_cols[:, b // 2, b % 2 : b % 2 + 1], ALU.add
+                per_sample = sample_weights["trait"]
             else:
-                i, g = s - B_STEPS, u
-                for k in range(2):
-                    rhs = x_words[g // 2][:, k, 1024 * (g % 2) : 1024 * (g % 2) + 1024]
+                i, g = step - B_STEPS, b
+                for k in range(VARIANT_GROUPS):
+                    x_bytes = x_words[g // 2][:, k, 2 * GROUP * (g % 2) : 2 * GROUP * (g % 2 + 1)]
                     nc.tensor.matmul_mx(
-                        out=ps[:], lhsT=w_codes[i][:, P * k : P * k + P].bitcast(FP8X4),
-                        lhsT_scale=w_scales[i][:, P * k : P * k + P],
-                        rhs=rhs.bitcast(FP4X4), rhs_scale=x_scales[:, k, N * g : N * g + N],
-                        start=(k == 0), stop=(k == 1),
+                        out=acc[:], lhsT=w_codes[i][:, P * k : P * (k + 1)].bitcast(FP8X4),
+                        lhsT_scale=w_scales[i][:, P * k : P * (k + 1)],
+                        rhs=x_bytes.bitcast(FP4X4), rhs_scale=x_scales[:, k, GROUP * g : GROUP * (g + 1)],
+                        start=(k == 0), stop=(k == VARIANT_GROUPS - 1),
                     )
-
-        def weigh(s, u, on_pool=False):
-            st = rt("staged", [P, N], BF16, 12)
-            staged[s, u] = st
-            if s < B_STEPS:
-                g, col, op0, wide = s, off_col[:, u // 2, u % 2 : u % 2 + 1], ALU.add, tw_wide
-            else:
-                i = s - B_STEPS
-                g, col, op0, wide = u, gs_col[:, i // 4, i % 4 : i % 4 + 1], ALU.mult, wides["pw"]
-            by_parity = mm_bank[s, u][:].rearrange("p (w u) -> p u w", u=2)
-            if on_pool:
-                shifted = rt("shifted", [P, N], F32, 2)
-                nc.scalar.activation(out=shifted[:].rearrange("p (u w) -> p u w", u=2), in_=by_parity,
-                                     func=ACT.Identity, bias=col)
-                nc.gpsimd.tensor_tensor(out=st[:], in0=shifted[:], in1=wide[:, N * g : N * g + N], op=ALU.mult)
-            else:
-                nc.vector.scalar_tensor_tensor(
-                    out=st[:].rearrange("p (u w) -> p u w", u=2), in0=by_parity, scalar=col,
-                    in1=wide[:, N * g : N * g + N].rearrange("p (u w) -> p u w", u=2),
-                    op0=op0, op1=ALU.mult,
-                )
-
-        def unit(s, u):
-            product(s, u)
-            weigh(s, u)
-
-        def turn(s):
-            gr = rt("grouped", [P, 4 * N], BF16, 6)
-            grouped[s] = gr
-            gr_words = gr[:].bitcast(F32).rearrange("p (c m u) -> p c m u", c=4, u=2)
-            for half in range(2):
-                ps = bank("tr", [P, 2, 2, P], TRB)
-                for cc in range(2):
-                    words = staged[s, 2 * half + cc][:].bitcast(F32)
-                    for u in range(2):
-                        nc.tensor.transpose(ps[:, cc, u, :], words[:, P * u : P * u + P], ident[:])
-                nc.scalar.copy(out=gr_words[:, 2 * half : 2 * half + 2, :, :], in_=ps[:].rearrange("p c u m -> p c m u"))
-
-        def step_quant(s, parts):
-            if s < B_STEPS:
-                cd = kt("b_codes%d" % s, [P, N], U32)
-                sc = kt("b_scales%d" % s, [P, N], U8)
-            else:
-                cd = rt("a_codes", [P, N], U32, 3)
-                sc = rt("a_scales", [P, N], U8, 3)
-            codes[s], scales[s] = cd, sc
-            w = N // parts
-            for part in range(parts):
-                quantize(cd[:, w * part : w * part + w], sc[:, w * part : w * part + w],
-                         grouped[s][:, 4 * w * part : 4 * w * part + 4 * w])
-
-        def z_passes(i, out, c0, c1):
-            s = i + B_STEPS
-            for g in range(4):
-                nc.tensor.matmul_mx(
-                    out=out, lhsT=codes[s][:, P * g : P * g + P].bitcast(FP8X4),
-                    lhsT_scale=scales[s][:, P * g : P * g + P],
-                    rhs=codes[g][:, c0:c1].bitcast(FP8X4), rhs_scale=scales[g][:, c0:c1],
-                    start=(g == 0), stop=(g == 3),
-                )
-
-        def z_whole(i):
-            ps = bank("z", [P, N], ZB)
-            zbank[i] = ps
-            z_passes(i, ps[:], 0, N)
-
-        def make_eg(i):
-            h, t = divmod(i, 4)
-            e = rt("eg", [P, R], F32, 4)
-            eg[i] = e
-            nc.scalar.activation(out=e[:], in_=e_raw[h][:, t, :], func=ACT.Copy, scale=gain_col[:, h, t : t + 1])
-
-        def z_out(i, ps_half, half):
-            h, t = divmod(i, 4)
-            cols = slice(256 * half, 256 * half + 256)
+                per_partition, first_op = gene_scale_cols[:, i // PACK, i % PACK : i % PACK + 1], ALU.mult
+                per_sample = sample_weights["pred"]
+            weighted[step, b] = rotating("weighted", [P, GROUP], BF16, 3 * BANKS)
             nc.vector.scalar_tensor_tensor(
-                out=y[h][:, t, cols].rearrange("p (m j) -> p m j", j=2),
-                in0=ps_half.rearrange("p (j m) -> p m j", j=2),
-                scalar=gain_col[:, h, t : t + 1],
-                in1=eg[i][:, cols].rearrange("p (m j) -> p m j", j=2),
+                out=weighted[step, b][:].rearrange("p (u w) -> p u w", u=2),
+                in0=acc[:].rearrange("p (w u) -> p u w", u=2),
+                scalar=per_partition,
+                in1=per_sample[:, GROUP * g : GROUP * (g + 1)].rearrange("p (u w) -> p u w", u=2),
+                op0=first_op, op1=ALU.mult,
+            )
+
+        def turn(step):
+            grouped[step] = rotating("grouped", [P, BANKS * GROUP], BF16, B_QUANTIZE_LAG - TURN_LAG + 1)
+            grouped_words = grouped[step][:].bitcast(F32).rearrange("p (b m u) -> p b m u", b=BANKS, u=2)
+            tag = "score" if step < B_STEPS and step % 2 == 1 else "turn"
+            for b0 in range(0, BANKS, 2):
+                turned = bank(tag, [P, 2, 2, P])
+                for b in range(2):
+                    words = weighted[step, b0 + b][:].bitcast(F32)
+                    for u in range(2):
+                        nc.tensor.transpose(turned[:, b, u, :], words[:, P * u : P * (u + 1)], ident[:])
+                nc.scalar.copy(out=grouped_words[:, b0 : b0 + 2, :, :], in_=turned[:].rearrange("p b u m -> p b m u"))
+
+        def quantize_step(step, parts=1):
+            if step < B_STEPS:
+                codes[step] = kept("b_codes%d" % step, [P, GROUP], U32)
+                scales[step] = kept("b_scales%d" % step, [P, GROUP], U8)
+            else:
+                codes[step] = rotating("a_codes", [P, GROUP], U32, 3)
+                scales[step] = rotating("a_scales", [P, GROUP], U8, 3)
+            width = GROUP // parts
+            for c0 in range(0, GROUP, width):
+                values = grouped[step][:, PACK * c0 : PACK * (c0 + width)]
+                quantize(codes[step][:, c0 : c0 + width], scales[step][:, c0 : c0 + width], values)
+
+        def score(i, acc, c0, c1):
+            a_step = B_STEPS + i
+            for g in range(SAMPLE_GROUPS):
+                nc.tensor.matmul_mx(
+                    out=acc, lhsT=codes[a_step][:, P * g : P * (g + 1)].bitcast(FP8X4),
+                    lhsT_scale=scales[a_step][:, P * g : P * (g + 1)],
+                    rhs=codes[g][:, c0:c1].bitcast(FP8X4), rhs_scale=scales[g][:, c0:c1],
+                    start=(g == 0), stop=(g == SAMPLE_GROUPS - 1),
+                )
+
+        def gain_earlier(i):
+            h, t = divmod(i, PACK)
+            earlier_gained[i] = rotating("earlier_gained", [P, TRAITS], F32, 4)
+            nc.scalar.activation(
+                out=earlier_gained[i][:], in_=earlier_raw[h][:, t, :], func=ACT.Copy, scale=gain_cols[:, h, t : t + 1]
+            )
+
+        def finish_half(i, acc, half):
+            h, t = divmod(i, PACK)
+            cols = slice(HALF * half, HALF * (half + 1))
+            nc.vector.scalar_tensor_tensor(
+                out=y[h][:, t, cols].rearrange("p (m c) -> p m c", c=2),
+                in0=acc.rearrange("p (c m) -> p m c", c=2),
+                scalar=gain_cols[:, h, t : t + 1],
+                in1=earlier_gained[i][:, cols].rearrange("p (m c) -> p m c", c=2),
                 op0=ALU.mult, op1=ALU.add,
             )
 
         def store_y(i, c0, c1):
-            h, t = divmod(i, 4)
-            rows = out_0[512 * h : 512 * h + 512, :].rearrange("(p t) r -> p t r", t=4)
+            h, t = divmod(i, PACK)
+            rows = out_0[GROUP * h : GROUP * (h + 1), :].rearrange("(p t) r -> p t r", t=PACK)
             nc.sync.dma_start(out=rows[:, t, c0:c1], in_=y[h][:, t, c0:c1])
 
-        def y_copy(engine_copy, h, c0, c1):
-            engine_copy(out=y_grouped[h][:, c0:c1, :], in_=y[h][:, :, c0:c1].rearrange("p t r -> p r t"))
+        def group_y(copy, h, c0, c1):
+            copy(out=y_grouped[h][:, c0:c1, :], in_=y[h][:, :, c0:c1].rearrange("p t r -> p r t"))
 
-        def y_quant(h, c0, c1):
-            quantize(y_codes[h][:, c0:c1], y_scales[h][:, c0:c1],
-                     y_grouped[h][:, c0:c1, :].rearrange("p r t -> p (r t)"))
+        def quantize_y(h, c0, c1):
+            values = y_grouped[h][:, c0:c1, :].rearrange("p r t -> p (r t)")
+            quantize(y_codes[h][:, c0:c1], y_scales[h][:, c0:c1], values)
+            dst = out_1[h].rearrange("p m t -> p (m t)")[:, PACK * c0 : PACK * c1]
+            nc.sync.dma_start(out=dst.bitcast(I32), in_=y_codes[h][:, c0:c1].bitcast(I32))
 
-        def store_words(h, c0, c1):
-            dst = out_1[h].rearrange("p m t -> p (m t)")
-            nc.sync.dma_start(out=dst[:, 4 * c0 : 4 * c1].bitcast(I32), in_=y_codes[h][:, c0:c1].bitcast(I32))
-
-        def store_scales(h, queues):
+        def store_y_scales(h, queues):
             for q in range(4):
-                queues[q].dma_start(
+                queues[q % len(queues)].dma_start(
                     out=out_2[h, 4 * q : 4 * q + 4, :].bitcast(I32),
                     in_=y_scales[h][32 * q : 32 * q + 4, :].bitcast(I32),
                 )
 
-        steps = B_STEPS + A_STEPS
-        last = A_STEPS - 1
-        for tick in range(steps + 2):
-            i_out = tick - 3 - B_STEPS
-            early = tick <= 4
-            if early:
-                unit(tick, 0)
-            for sq in range(steps - 1):
-                if tick == ((4,5,6,6)[sq] if sq < B_STEPS else sq + 2):
-                    step_quant(sq, 1)
-            if tick - 2 == steps - 1:
-                step_quant(tick - 2, 2)
-            if tick == 3:
-                w_quant(0)
-            if 0 <= i_out < last:
-                for half in range(2):
-                    z_out(i_out, zbank[i_out][:, 256 * half : 256 * half + 256], half)
-                store_y(i_out, 0, R)
-            if tick in (10, 11):
-                y_copy(nc.scalar.copy, 0, 256 * (tick - 10), 256 * (tick - 10) + 256)
-            if tick < steps:
-                if not early:
-                    unit(tick, 0)
-                unit(tick, 1)
-                if 1 <= tick - 3 < A_STEPS:
-                    w_quant(tick - 3)
-                unit(tick, 2)
-                unit(tick, 3)
-            if tick == 11:
-                y_quant(0, 0, R)
-                store_words(0, 0, R)
-                store_scales(0, [nc.sync] * 4)
-            if 0 <= tick - 1 < steps:
-                turn(tick - 1)
-            if tick == 0:
-                wides["pw"] = spread(pw_rows, "pw_wide", "z", [(0, 4)])
-            if tick <= 1:
-                w_copy(0, tick)
-            if 3 <= tick <= 8:
-                w_copy((tick - 1) // 2, (tick - 1) % 2)
-            if tick == 4:
-                nc.scalar.activation(out=gain_col[:], in_=gain_raw[:], func=ACT.Copy)
-            if 0 <= tick - 5 < A_STEPS:
-                make_eg(tick - 5)
-            i_z = tick - 2 - B_STEPS
-            if 0 <= i_z < last:
-                z_whole(i_z)
+        last_tile = GENE_TILES - 1
+        first_group_done = B_STEPS + PACK - 1 + FINISH_LAG
+        for tick in range(STEPS + SCORE_LAG):
+            a_step = tick - SCORE_LAG
+            if a_step >= B_STEPS:
+                quantize_step(a_step, 2 if a_step == STEPS - 1 else 1)
+            for g in range(B_STEPS):
+                if tick == min(g + B_QUANTIZE_LAG, FIRST_SCORE_TICK):
+                    quantize_step(g)
 
+            finished = tick - FINISH_LAG - B_STEPS
+            if finished >= 0:
+                for half in range(2):
+                    finish_half(finished, score_banks[finished][:, HALF * half : HALF * (half + 1)], half)
+                store_y(finished, 0, TRAITS)
+            y_half = tick - first_group_done
+            if y_half in (0, 1):
+                group_y(nc.scalar.copy, 0, HALF * y_half, HALF * (y_half + 1))
+
+            if tick < STEPS:
+                product(tick, 0)
+                next_tile = tick + 1 - B_STEPS
+                if 0 <= next_tile < GENE_TILES:
+                    quantize_w(next_tile)
+                for b in range(1, BANKS):
+                    product(tick, b)
+            if y_half == 1:
+                quantize_y(0, 0, TRAITS)
+                store_y_scales(0, [nc.sync])
+
+            if 0 <= tick - TURN_LAG < STEPS:
+                turn(tick - TURN_LAG)
+            if tick == 0:
+                sample_weights["pred"] = spread(
+                    pred_weight_rows, "pred_weight_wide", "score", nc.scalar.copy, [(0, SAMPLE_GROUPS)]
+                )
+            if tick < GENE_TILES:
+                group_w(tick // VARIANT_GROUPS, tick % VARIANT_GROUPS)
+            scored = tick - FIRST_SCORE_TICK
+            if scored == -2:
+                nc.scalar.activation(out=gain_cols[:], in_=gain_raw[:], func=ACT.Copy)
+            if 0 <= scored + 1 < GENE_TILES:
+                gain_earlier(scored + 1)
+            if 0 <= scored < last_tile:
+                score_banks[scored] = bank("score", [P, TRAITS])
+                score(scored, score_banks[scored][:], 0, TRAITS)
+
+        h = GENE_GROUPS - 1
         halves = []
         for half in range(2):
-            ps = bank("mm", [P, N], MMB)
-            z_passes(last, ps[:, 0:256], 256 * half, 256 * half + 256)
-            halves.append(ps)
-        z_out(last, halves[0][:, 0:256], 0)
-        store_y(last, 0, 256)
-        y_copy(nc.scalar.copy, 1, 0, 128)
-        y_copy(nc.vector.tensor_copy, 1, 128, 256)
-        z_out(last, halves[1][:, 0:256], 1)
-        store_y(last, 256, R)
-        y_copy(nc.scalar.copy, 1, 256, 384)
-        y_quant(1, 0, 256)
-        store_words(1, 0, 256)
-        y_copy(nc.vector.tensor_copy, 1, 384, R)
-        y_quant(1, 256, R)
-        store_words(1, 256, R)
-        store_scales(1, [nc.scalar, nc.sync, nc.scalar, nc.sync])
+            acc = bank("product", [P, GROUP])
+            score(last_tile, acc[:, 0:HALF], HALF * half, HALF * (half + 1))
+            halves.append(acc[:, 0:HALF])
+        finish_half(last_tile, halves[0], 0)
+        store_y(last_tile, 0, HALF)
+        group_y(nc.scalar.copy, h, 0, QUARTER)
+        group_y(nc.vector.tensor_copy, h, QUARTER, HALF)
+        finish_half(last_tile, halves[1], 1)
+        store_y(last_tile, HALF, TRAITS)
+        group_y(nc.scalar.copy, h, HALF, HALF + QUARTER)
+        quantize_y(h, 0, HALF)
+        group_y(nc.vector.tensor_copy, h, HALF + QUARTER, TRAITS)
+        quantize_y(h, HALF, TRAITS)
+        store_y_scales(h, [nc.scalar, nc.sync])

from contextlib import ExitStack

import concourse.mybir as mybir
from concourse.masks import make_identity

SAMPLES, VARIANTS, GENES, MEASURES, TRAITS = 2048, 1024, 1024, 512, 512
FLOPS = 2 * (SAMPLES * VARIANTS * GENES + SAMPLES * MEASURES * TRAITS + GENES * TRAITS * SAMPLES)

F32 = mybir.dt.float32
BF16 = mybir.dt.bfloat16
I32 = mybir.dt.int32
U32 = mybir.dt.uint32
U8 = mybir.dt.uint8
FP8X4 = mybir.dt.float8_e4m3fn_x4
FP4X4 = mybir.dt.float4_e2m1fn_x4
ALU = mybir.AluOpType
ACT = mybir.ActivationFunctionType

P = 128
PACK = 4
GROUP = P * PACK
SAMPLE_GROUPS = SAMPLES // GROUP
VARIANT_GROUPS = VARIANTS // GROUP
GENE_GROUPS = GENES // GROUP
GENE_TILES = GENES // P
TRAIT_TILES = TRAITS // P
HALF = TRAITS // 2
QUARTER = TRAITS // 4

BANKS = 4
B_STEPS = SAMPLE_GROUPS
STEPS = B_STEPS + GENE_TILES

TURN_LAG = 1
SCORE_LAG = 2
FINISH_LAG = 3
FIRST_SCORE_TICK = B_STEPS + SCORE_LAG
B_QUANTIZE_LAG = 4


def tile_transcriptome_association_scores_k4_kernel(
    tc, geno_words, geno_scales, expr_w, gene_scale, pred_weight, meas_words, meas_scales,
    loadings, offset, trait_weight, earlier, gene_gain, out_0, out_1, out_2,
):
    nc = tc.nc
    with ExitStack() as ctx:
        keep = ctx.enter_context(tc.tile_pool(name="keep", bufs=1))
        ring = ctx.enter_context(tc.tile_pool(name="ring", bufs=1))
        psum = ctx.enter_context(tc.psum_pool(name="psum", bufs=1))
        ctx.enter_context(tc.manual_schedule())

        def kept(name, shape, dtype):
            return keep.tile(shape, dtype, name=name, align_bytes=64)

        def kept_list(name, count, shape, dtype):
            return [kept("%s%d" % (name, n), shape, dtype) for n in range(count)]

        def rotating(tag, shape, dtype, bufs):
            return ring.tile(shape, dtype, name=tag, tag=tag, bufs=bufs, align_bytes=64)

        psum_banks = {"product": BANKS, "turn": 2, "score": 2}

        def bank(tag, shape):
            return psum.tile(shape, F32, name=tag, tag=tag, bufs=psum_banks[tag])

        def quantize(codes, scales, values):
            nc.vector.quantize_mx(out=codes.bitcast(FP8X4), scales=scales, in_=values)

        p_scales = kept("p_scales", [P, SAMPLES], U8)
        x_scales = kept("x_scales", [P, VARIANT_GROUPS, SAMPLES], U8)
        nc.vector.memset(p_scales[:].bitcast(I32), 0)
        nc.vector.memset(x_scales[:].rearrange("p k n -> p (k n)").bitcast(I32), 0)

        per_row = SAMPLES // P
        trait_weight_rows = kept("trait_weight_rows", [P, per_row], BF16)
        pred_weight_rows = kept("pred_weight_rows", [P, per_row], BF16)
        offset_cols = kept("offset_cols", [P, 2, 2], BF16)
        gene_scale_cols = kept("gene_scale_cols", [P, GENE_GROUPS, PACK], BF16)
        gain_raw = kept("gain_raw", [P, GENE_GROUPS, PACK], BF16)
        l_raw = kept("l_raw", [P, PACK, TRAITS], BF16)
        w_raw = kept_list("w_raw", GENE_GROUPS, [P, VARIANT_GROUPS, PACK, GROUP], BF16)
        p_words = kept_list("p_words", SAMPLE_GROUPS, [P, GROUP], U32)
        x_words = kept_list("x_words", 2, [P, VARIANT_GROUPS, SAMPLES], U8)
        earlier_raw = kept_list("earlier_raw", GENE_GROUPS, [P, PACK, TRAITS], BF16)

        def load_p(g):
            flat = meas_words[0].rearrange("p n t -> p (n t)")
            src = flat[:, PACK * GROUP * g : PACK * GROUP * (g + 1)]
            nc.sync.dma_start(out=p_words[g][:].bitcast(I32), in_=src.bitcast(I32))

        def load_w(h, k):
            src = expr_w[GROUP * k : GROUP * (k + 1), GROUP * h : GROUP * (h + 1)]
            nc.sync.dma_start(out=w_raw[h][:, k, :, :], in_=src.rearrange("(p t) c -> p t c", t=PACK))

        def load_x(half):
            src = geno_words[:, :, SAMPLES * half : SAMPLES * (half + 1)]
            nc.sync.dma_start(out=x_words[half][:].bitcast(I32), in_=src.rearrange("k p b -> p k b").bitcast(I32))

        def load_gene_cols(cols, vector):
            nc.sync.dma_start(out=cols[:], in_=vector.rearrange("(h p t) -> p h t", h=GENE_GROUPS, t=PACK))

        nc.sync.dma_start(out=trait_weight_rows[:], in_=trait_weight.rearrange("(p m) -> p m", m=per_row))
        nc.sync.dma_start(out=l_raw[:], in_=loadings.rearrange("(p t) c -> p t c", t=PACK))
        for q in range(4):
            nc.scalar.dma_start(
                out=p_scales[32 * q : 32 * q + 4, :].bitcast(I32),
                in_=meas_scales[0, 4 * q : 4 * q + 4, :].bitcast(I32),
            )
        load_p(0)
        nc.sync.dma_start(out=offset_cols[:], in_=offset.rearrange("(h p c) -> p h c", h=2, c=2))
        nc.sync.dma_start(out=pred_weight_rows[:], in_=pred_weight.rearrange("(p m) -> p m", m=per_row))
        load_p(1)
        load_w(0, 0)
        load_p(2)
        load_w(0, 1)
        load_p(3)
        for q in range(4):
            nc.sync.dma_start(
                out=x_scales[32 * q : 32 * q + 4, :, :].bitcast(I32),
                in_=geno_scales[:, 4 * q : 4 * q + 4, :].rearrange("k r n -> r k n").bitcast(I32),
            )
        load_x(0)
        load_gene_cols(gene_scale_cols, gene_scale)
        load_x(1)
        load_w(1, 0)
        load_w(1, 1)
        load_gene_cols(gain_raw, gene_gain)
        for h in range(GENE_GROUPS):
            src = earlier[GROUP * h : GROUP * (h + 1), :]
            nc.sync.dma_start(out=earlier_raw[h][:], in_=src.rearrange("(p t) r -> p t r", t=PACK))

        ident = kept("ident", [P, P], F32)
        make_identity(nc, ident[:])
        warm = kept("warm", [P, 1], F32)
        nc.scalar.activation(out=warm[:], in_=ident[:, 0:1], func=ACT.Copy)

        def spread(rows, name, tag, sort_copy, group_ranges):
            by_parity = kept(name + "_sorted", [P, 2, per_row // 2], BF16)
            sort_copy(out=by_parity[:], in_=rows[:].rearrange("p (w u) -> p u w", u=2))
            words = by_parity[:].bitcast(F32)
            wide = kept(name, [P, SAMPLES], BF16)
            wide_words = wide[:].bitcast(F32).rearrange("p (g u n c) -> p u g n c", g=SAMPLE_GROUPS, u=2, c=4)
            banks = []
            for u in range(2):
                spread_bank = bank(tag, [P, 4, P])
                banks.append(spread_bank[:].rearrange("p c (g n) -> p g n c", g=SAMPLE_GROUPS))
                for c in range(4):
                    nc.tensor.transpose(spread_bank[:, c, :], words[:, u, c : c + 1].to_broadcast([P, P]), ident[:])
            for g0, g1 in group_ranges:
                for u in range(2):
                    nc.scalar.copy(out=wide_words[:, u, g0:g1, :, :], in_=banks[u][:, g0:g1, :, :])
            return wide

        l_grouped = kept_list("l_grouped", TRAIT_TILES, [P, P, PACK], BF16)
        l_codes = kept_list("l_codes", TRAIT_TILES, [P, P], U32)
        l_scales = kept_list("l_scales", TRAIT_TILES, [P, P], U8)

        def group_l(copy, j):
            src = l_raw[:].rearrange("p t (h m c) -> p h c m t", h=2, c=2)
            copy(out=l_grouped[j][:], in_=src[:, j // 2, j % 2, :, :])

        def quantize_l(j):
            quantize(l_codes[j][:], l_scales[j][:], l_grouped[j][:].rearrange("p m t -> p (m t)"))

        group_l(nc.scalar.copy, 1)
        sample_weights = {}
        sample_weights["trait"] = spread(
            trait_weight_rows, "trait_weight_wide", "turn", nc.vector.tensor_copy, [(0, 1), (1, SAMPLE_GROUPS)]
        )
        group_l(nc.vector.tensor_copy, 0)
        quantize_l(0)
        quantize_l(1)
        group_l(nc.vector.tensor_copy, 2)
        group_l(nc.vector.tensor_copy, 3)
        quantize_l(2)
        quantize_l(3)

        gain_cols = kept("gain_cols", [P, GENE_GROUPS, PACK], F32)
        y = kept_list("y", GENE_GROUPS, [P, PACK, TRAITS], F32)
        y_grouped = kept_list("y_grouped", GENE_GROUPS, [P, TRAITS, PACK], BF16)
        y_codes = kept_list("y_codes", GENE_GROUPS, [P, TRAITS], U32)
        y_scales = kept_list("y_scales", GENE_GROUPS, [P, TRAITS], U8)
        w_grouped, w_codes, w_scales = {}, {}, {}
        weighted, grouped, codes, scales = {}, {}, {}, {}
        earlier_gained, score_banks = {}, {}

        def group_w(pair, k):
            h, first = pair // 2, 2 * (pair % 2)
            if k == 0:
                w_grouped[pair] = rotating("w_grouped", [P, 2, VARIANT_GROUPS, P, PACK], BF16, 2)
            src = w_raw[h][:, k, :, :].rearrange("p j (m t) -> p m t j", t=PACK)
            dst = w_grouped[pair][:, :, k, :, :].rearrange("p t m j -> p m t j")
            nc.scalar.copy(out=dst, in_=src[:, :, first : first + 2, :])

        def quantize_w(i):
            w_codes[i] = rotating("w_codes", [P, VARIANT_GROUPS * P], U32, 3)
            w_scales[i] = rotating("w_scales", [P, VARIANT_GROUPS * P], U8, 3)
            values = w_grouped[i // 2][:, i % 2, :, :, :].rearrange("p k m j -> p (k m j)")
            quantize(w_codes[i][:], w_scales[i][:], values)

        def product(step, b):
            acc = bank("product", [P, GROUP])
            if step < B_STEPS:
                g = step
                nc.tensor.matmul_mx(
                    out=acc[:], lhsT=l_codes[b][:].bitcast(FP8X4), lhsT_scale=l_scales[b][:],
                    rhs=p_words[g][:].bitcast(FP8X4), rhs_scale=p_scales[:, GROUP * g : GROUP * (g + 1)],
                    start=True, stop=True,
                )
                per_partition, first_op = offset_cols[:, b // 2, b % 2 : b % 2 + 1], ALU.add
                per_sample = sample_weights["trait"]
            else:
                i, g = step - B_STEPS, b
                for k in range(VARIANT_GROUPS):
                    x_bytes = x_words[g // 2][:, k, 2 * GROUP * (g % 2) : 2 * GROUP * (g % 2 + 1)]
                    nc.tensor.matmul_mx(
                        out=acc[:], lhsT=w_codes[i][:, P * k : P * (k + 1)].bitcast(FP8X4),
                        lhsT_scale=w_scales[i][:, P * k : P * (k + 1)],
                        rhs=x_bytes.bitcast(FP4X4), rhs_scale=x_scales[:, k, GROUP * g : GROUP * (g + 1)],
                        start=(k == 0), stop=(k == VARIANT_GROUPS - 1),
                    )
                per_partition, first_op = gene_scale_cols[:, i // PACK, i % PACK : i % PACK + 1], ALU.mult
                per_sample = sample_weights["pred"]
            weighted[step, b] = rotating("weighted", [P, GROUP], BF16, 3 * BANKS)
            nc.vector.scalar_tensor_tensor(
                out=weighted[step, b][:].rearrange("p (u w) -> p u w", u=2),
                in0=acc[:].rearrange("p (w u) -> p u w", u=2),
                scalar=per_partition,
                in1=per_sample[:, GROUP * g : GROUP * (g + 1)].rearrange("p (u w) -> p u w", u=2),
                op0=first_op, op1=ALU.mult,
            )

        def turn(step):
            grouped[step] = rotating("grouped", [P, BANKS * GROUP], BF16, B_QUANTIZE_LAG - TURN_LAG + 1)
            grouped_words = grouped[step][:].bitcast(F32).rearrange("p (b m u) -> p b m u", b=BANKS, u=2)
            tag = "score" if step < B_STEPS and step % 2 == 1 else "turn"
            for b0 in range(0, BANKS, 2):
                turned = bank(tag, [P, 2, 2, P])
                for b in range(2):
                    words = weighted[step, b0 + b][:].bitcast(F32)
                    for u in range(2):
                        nc.tensor.transpose(turned[:, b, u, :], words[:, P * u : P * (u + 1)], ident[:])
                nc.scalar.copy(out=grouped_words[:, b0 : b0 + 2, :, :], in_=turned[:].rearrange("p b u m -> p b m u"))

        def quantize_step(step, parts=1):
            if step < B_STEPS:
                codes[step] = kept("b_codes%d" % step, [P, GROUP], U32)
                scales[step] = kept("b_scales%d" % step, [P, GROUP], U8)
            else:
                codes[step] = rotating("a_codes", [P, GROUP], U32, 3)
                scales[step] = rotating("a_scales", [P, GROUP], U8, 3)
            width = GROUP // parts
            for c0 in range(0, GROUP, width):
                values = grouped[step][:, PACK * c0 : PACK * (c0 + width)]
                quantize(codes[step][:, c0 : c0 + width], scales[step][:, c0 : c0 + width], values)

        def score(i, acc, c0, c1):
            a_step = B_STEPS + i
            for g in range(SAMPLE_GROUPS):
                nc.tensor.matmul_mx(
                    out=acc, lhsT=codes[a_step][:, P * g : P * (g + 1)].bitcast(FP8X4),
                    lhsT_scale=scales[a_step][:, P * g : P * (g + 1)],
                    rhs=codes[g][:, c0:c1].bitcast(FP8X4), rhs_scale=scales[g][:, c0:c1],
                    start=(g == 0), stop=(g == SAMPLE_GROUPS - 1),
                )

        def gain_earlier(i):
            h, t = divmod(i, PACK)
            earlier_gained[i] = rotating("earlier_gained", [P, TRAITS], F32, 4)
            nc.scalar.activation(
                out=earlier_gained[i][:], in_=earlier_raw[h][:, t, :], func=ACT.Copy, scale=gain_cols[:, h, t : t + 1]
            )

        def finish_half(i, acc, half):
            h, t = divmod(i, PACK)
            cols = slice(HALF * half, HALF * (half + 1))
            nc.vector.scalar_tensor_tensor(
                out=y[h][:, t, cols].rearrange("p (m c) -> p m c", c=2),
                in0=acc.rearrange("p (c m) -> p m c", c=2),
                scalar=gain_cols[:, h, t : t + 1],
                in1=earlier_gained[i][:, cols].rearrange("p (m c) -> p m c", c=2),
                op0=ALU.mult, op1=ALU.add,
            )

        def store_y(i, c0, c1):
            h, t = divmod(i, PACK)
            rows = out_0[GROUP * h : GROUP * (h + 1), :].rearrange("(p t) r -> p t r", t=PACK)
            nc.sync.dma_start(out=rows[:, t, c0:c1], in_=y[h][:, t, c0:c1])

        def group_y(copy, h, c0, c1):
            copy(out=y_grouped[h][:, c0:c1, :], in_=y[h][:, :, c0:c1].rearrange("p t r -> p r t"))

        def quantize_y(h, c0, c1):
            values = y_grouped[h][:, c0:c1, :].rearrange("p r t -> p (r t)")
            quantize(y_codes[h][:, c0:c1], y_scales[h][:, c0:c1], values)
            dst = out_1[h].rearrange("p m t -> p (m t)")[:, PACK * c0 : PACK * c1]
            nc.sync.dma_start(out=dst.bitcast(I32), in_=y_codes[h][:, c0:c1].bitcast(I32))

        def store_y_scales(h, queues):
            for q in range(4):
                queues[q % len(queues)].dma_start(
                    out=out_2[h, 4 * q : 4 * q + 4, :].bitcast(I32),
                    in_=y_scales[h][32 * q : 32 * q + 4, :].bitcast(I32),
                )

        last_tile = GENE_TILES - 1
        first_group_done = B_STEPS + PACK - 1 + FINISH_LAG
        for tick in range(STEPS + SCORE_LAG):
            a_step = tick - SCORE_LAG
            if a_step >= B_STEPS:
                quantize_step(a_step, 2 if a_step == STEPS - 1 else 1)
            for g in range(B_STEPS):
                if tick == min(g + B_QUANTIZE_LAG, FIRST_SCORE_TICK):
                    quantize_step(g)

            finished = tick - FINISH_LAG - B_STEPS
            if finished >= 0:
                for half in range(2):
                    finish_half(finished, score_banks[finished][:, HALF * half : HALF * (half + 1)], half)
                store_y(finished, 0, TRAITS)
            y_half = tick - first_group_done
            if y_half in (0, 1):
                group_y(nc.scalar.copy, 0, HALF * y_half, HALF * (y_half + 1))

            if tick < STEPS:
                product(tick, 0)
                next_tile = tick + 1 - B_STEPS
                if 0 <= next_tile < GENE_TILES:
                    quantize_w(next_tile)
                for b in range(1, BANKS):
                    product(tick, b)
            if y_half == 1:
                quantize_y(0, 0, TRAITS)
                store_y_scales(0, [nc.sync])

            if 0 <= tick - TURN_LAG < STEPS:
                turn(tick - TURN_LAG)
            if tick == 0:
                sample_weights["pred"] = spread(
                    pred_weight_rows, "pred_weight_wide", "score", nc.scalar.copy, [(0, SAMPLE_GROUPS)]
                )
            if tick < GENE_TILES:
                group_w(tick // VARIANT_GROUPS, tick % VARIANT_GROUPS)
            scored = tick - FIRST_SCORE_TICK
            if scored == -2:
                nc.scalar.activation(out=gain_cols[:], in_=gain_raw[:], func=ACT.Copy)
            if 0 <= scored + 1 < GENE_TILES:
                gain_earlier(scored + 1)
            if 0 <= scored < last_tile:
                score_banks[scored] = bank("score", [P, TRAITS])
                score(scored, score_banks[scored][:], 0, TRAITS)

        h = GENE_GROUPS - 1
        halves = []
        for half in range(2):
            acc = bank("product", [P, GROUP])
            score(last_tile, acc[:, 0:HALF], HALF * half, HALF * (half + 1))
            halves.append(acc[:, 0:HALF])
        finish_half(last_tile, halves[0], 0)
        store_y(last_tile, 0, HALF)
        group_y(nc.scalar.copy, h, 0, QUARTER)
        group_y(nc.vector.tensor_copy, h, QUARTER, HALF)
        finish_half(last_tile, halves[1], 1)
        store_y(last_tile, HALF, TRAITS)
        group_y(nc.scalar.copy, h, HALF, HALF + QUARTER)
        quantize_y(h, 0, HALF)
        group_y(nc.vector.tensor_copy, h, HALF + QUARTER, TRAITS)
        quantize_y(h, HALF, TRAITS)
        store_y_scales(h, [nc.scalar, nc.sync])
